import numpy as np
import ml_dtypes


def mxq(x, axis, fmt="e4m3"):
    dtype, down = {"e4m3": (ml_dtypes.float8_e4m3fn, 7), "e5m2": (ml_dtypes.float8_e5m2, 14)}[fmt]
    v = np.moveaxis(np.asarray(x, np.float32).astype(ml_dtypes.bfloat16).astype(np.float64), axis, -1)
    blocks = v.reshape(v.shape[:-1] + (-1, 32))
    amax = np.abs(blocks).max(-1, keepdims=True)
    byte = np.maximum(np.where(amax > 0, np.frexp(amax)[1] - 1 + 127, 0) - down, 1)
    scale = np.exp2(byte - 127.0)
    codes = (blocks / scale).astype(np.float32).astype(dtype).astype(np.float64)
    return np.moveaxis((codes * scale).reshape(v.shape), -1, axis)


WIDE = False


def mx_kscale(k):
    if not WIDE:
        return np.ones(k)
    levels = np.array([10, -10, 5, -5, 0])
    if k % 512:
        return np.exp2(np.random.permutation(np.resize(levels, k // 32))).repeat(32)
    a = np.empty((k // 512, 16))
    for p in range(k // 512):
        a[p, :8] = np.random.permutation(np.resize(levels, 8))
        for g in range(8):
            far = levels[np.abs(levels - a[p, g]) >= 10]
            a[p, g + 8] = far[np.random.randint(len(far))]
    return np.exp2(a.ravel()).repeat(32)


def f64(x):
    return np.asarray(x).astype(np.float64)


def striped(idx):
    return np.tile(idx.reshape(-1, 16).T, (8, 1)).astype(np.uint16)


def unstriped(offs):
    return offs[:16].T.reshape(-1).astype(np.int64)


def striped8(idx):
    return np.concatenate([x.reshape(-1, 16).T for x in idx]).astype(np.uint16)


def runs(offs, k):
    lists = np.stack([offs[16 * r : 16 * r + 16].T.reshape(-1) for r in range(8)]).astype(np.int64)
    return lists[np.arange(k) % 512 // 64]


def pack_weight(w):
    k, n = w.shape
    w = f64(np.asarray(w, np.float32).astype(ml_dtypes.bfloat16)).reshape(k // 32, 32, n)
    amax = np.abs(w).max(1)
    byte = np.clip(np.where(amax > 0, np.frexp(amax)[1] - 1 + 127 - 7, 1), 1, 254)
    scaled = (w * np.exp2(127.0 - byte)[:, None, :]).reshape(k, n).astype(np.float32)
    words = np.ascontiguousarray(scaled.reshape(k // 512, 128, 4, n).transpose(0, 1, 3, 2)).astype(ml_dtypes.float8_e4m3fn).view(np.uint8)
    return words, np.ascontiguousarray(byte.astype(np.uint8).reshape(k // 512, 16, n))


def unpack_weight(words, scales):
    g, p, n, _ = words.shape
    vals = np.ascontiguousarray(words).view(ml_dtypes.float8_e4m3fn).astype(np.float64) * np.repeat(np.exp2(scales.astype(np.float64) - 127.0), 8, axis=1)[..., None]
    return vals.transpose(0, 1, 3, 2).reshape(g * 512, n)


K, T, S, H, J, C = 512, 2048, 512, 512, 512, 512


def setup_inputs():
    n = np.random.standard_normal
    s = mx_kscale(K)[:, None]
    packed_xT = pack_weight(n((K, T)) * s)
    return {
        "x_words": packed_xT[0],
        "x_scales": packed_xT[1],
        "w1": (n((K, H)) / np.sqrt(K) / s).astype(np.float32),
        "tab": n((H, J)).astype(np.float32),
        "gs": (np.random.uniform(0.5, 1.5, (K, 1)) / s).astype(np.float32),
        "offs": striped(np.random.permutation(T)[:S]),
        "n1": striped8(np.random.randint(0, J, (8, S))),
        "n2": striped8(np.random.randint(0, J, (8, S))),
        "n3": striped8(np.stack([np.random.permutation(S) for _ in range(8)])),
        "cand": striped(np.random.permutation(T)[:C]),
        "n4": striped8(np.stack([np.random.permutation(S) for _ in range(8)])),
        "n5": striped8(np.stack([np.random.permutation(S) for _ in range(8)])),
        "n6": striped8(np.stack([np.random.permutation(S) for _ in range(8)])),
    }


def reference(x_words, x_scales, w1, tab, gs, offs, n1, n2, n3, cand, n4, n5, n6):
    x_cand = unpack_weight(x_words, x_scales)[:, unstriped(cand)]
    xq = unpack_weight(x_words, x_scales)[:, unstriped(offs)]
    y = mxq(f64(w1), 0, "e4m3").T @ xq
    z = f64(gs) * ((y[np.arange(H)[:, None], runs(n3, H)]) * (f64(tab)[np.arange(H)[:, None], runs(n1, H)]) + f64(tab)[np.arange(H)[:, None], runs(n2, H)])
    s = 0.0625 * ((x_cand.T @ mxq(z, 0, "e4m3")))
    return s + s[np.arange(C)[:, None], runs(n4, C)] - (np.maximum(s[np.arange(C)[:, None], runs(n5, C)], s[np.arange(C)[:, None], runs(n6, C)]))

@@ -1,0 +1,158 @@
+from contextlib import ExitStack
+
+import concourse.mybir as mybir
+
+F32 = mybir.dt.float32
+BF16 = mybir.dt.bfloat16
+I32 = mybir.dt.int32
+U32 = mybir.dt.uint32
+U16 = mybir.dt.uint16
+U8 = mybir.dt.uint8
+FP8X4 = mybir.dt.float8_e4m3fn_x4
+ALU = mybir.AluOpType
+COPY = mybir.ActivationFunctionType.Copy
+
+P = 128
+T = 2048
+N = 512
+PACK = 4
+WIN = 2 * N
+HALF = N // 2
+FLOPS = 2 * 2 * 512 * 512 * 512
+
+
+def tile_picked_candkindatrim_none_p_kernel(tc, x_words, x_scales, w1, tab, gs, offs, n1, n2, n3, cand, n4, n5, n6, out):
+    nc = tc.nc
+    with ExitStack() as ctx:
+        lists = ctx.enter_context(tc.tile_pool(name="lists", bufs=1))
+        keep = ctx.enter_context(tc.tile_pool(name="keep", bufs=1))
+        psum = ctx.enter_context(tc.psum_pool(name="psum", bufs=1))
+
+        def load_list(src, name):
+            tile = lists.tile([P, N // 16], U16, name=name)
+            nc.sync.dma_start(tile[:], src)
+            return tile
+
+        xs = keep.tile([P, T], U8, name="xs", align_bytes=64)
+        nc.vector.memset(xs[:].bitcast(I32), 0)
+
+        tab_rows = tab.rearrange("(p t) c -> p t c", t=PACK)
+        tabw = [keep.tile([P, WIN], F32, name="tabw%d" % t) for t in range(PACK)]
+        l1 = load_list(n1, "l1")
+        gs_t = keep.tile([P, PACK], F32, name="gs_t")
+        for t in range(PACK):
+            nc.sync.dma_start(tabw[t][:, :N], tab_rows[:, t, :])
+            if t == 0:
+                nc.sync.dma_start(gs_t[:], gs.rearrange("(p t) o -> p (t o)", t=PACK))
+        w_rows = w1.rearrange("(p j) c -> p j c", j=PACK)
+        wraw = [keep.tile([P, PACK, HALF], F32, name="wraw%d" % h) for h in range(2)]
+        for h in range(2):
+            nc.sync.dma_start(wraw[h][:], w_rows[:, :, h * HALF:(h + 1) * HALF])
+        for q in range(4):
+            nc.scalar.dma_start(xs[32 * q:32 * q + 4, :].bitcast(I32), x_scales[0, 4 * q:4 * q + 4, :].bitcast(I32))
+        loffs = load_list(offs, "loffs")
+        xw = keep.tile([P, T], U32, name="xw", align_bytes=64)
+        nc.sync.dma_start(xw[:].bitcast(I32), x_words[0].rearrange("p c r -> p (c r)").bitcast(I32))
+        lcand = load_list(cand, "lcand")
+        l3 = load_list(n3, "l3")
+        l2 = load_list(n2, "l2")
+        l4 = load_list(n4, "l4")
+        l5 = load_list(n5, "l5")
+        l6 = load_list(n6, "l6")
+
+        g1 = [keep.tile([P, N], F32, name="g1_%d" % t, tag="g1_%d" % t) for t in range(PACK)]
+        for t in range(PACK):
+            nc.vector.tensor_copy(g1[t][:], tabw[t][:].indirect(l1[:]))
+
+        wb = keep.tile([P, PACK * N], BF16, name="wb", align_bytes=64)
+        wb_v = wb[:].rearrange("p (t m j) -> p m j t", t=PACK, j=PACK)
+        for h in range(2):
+            nc.scalar.copy(wb_v[:, h * 64:(h + 1) * 64], wraw[h][:].rearrange("p j (m t) -> p m j t", t=PACK))
+        xq_s = keep.tile([P, N], U8, name="xq_s", align_bytes=64)
+        nc.vector.tensor_copy(xq_s[:], xs[:].indirect(loffs[:]))
+        wq = keep.tile([P, N], U32, name="wq", align_bytes=64)
+        wsc = keep.tile([P, N], U8, name="wsc", align_bytes=64)
+        nc.vector.quantize_mx(out=wq[:].bitcast(FP8X4), scales=wsc[:], in_=wb[:])
+        xq_w = keep.tile([P, N], U32, name="xq_w", align_bytes=64)
+        nc.vector.tensor_copy(xq_w[:], xw[:].indirect(loffs[:]))
+        xc_s0 = keep.tile([P, N], U8, name="xc_s0", align_bytes=64)
+        nc.vector.tensor_copy(xc_s0[:], xs[:].indirect(lcand[:]))
+        xc_s = keep.tile([P, N], U8, name="xc_s", align_bytes=64)
+        nc.vector.tensor_copy(xc_s[:].bitcast(I32).rearrange("p (t a w) -> p t a w", t=PACK, w=2),
+                              xc_s0[:].bitcast(I32).rearrange("p (a t w) -> p t a w", t=PACK, w=2))
+
+        yw = [keep.tile([P, WIN], F32, name="yw%d" % t, tag="yw%d" % t) for t in range(PACK)]
+        for t in range(PACK):
+            cols = slice(t * P, (t + 1) * P)
+            acc = psum.tile([P, N], F32, name="yacc%d" % t)
+            nc.tensor.matmul_mx(out=acc[:], lhsT=wq[:, cols].bitcast(FP8X4), lhsT_scale=wsc[:, cols],
+                                rhs=xq_w[:].bitcast(FP8X4), rhs_scale=xq_s[:], start=True, stop=True)
+            nc.scalar.activation(yw[t][:, :N], acc[:], COPY, scale=gs_t[:, t:t + 1])
+        tgw = [keep.tile([P, WIN], F32, name="tgw%d" % t) for t in range(PACK)]
+        for t in range(PACK):
+            nc.scalar.activation(tgw[t][:, :N], tabw[t][:, :N], COPY, scale=gs_t[:, t:t + 1])
+
+        prod = [keep.tile([P, N], F32, name="prod%d" % t, tag="prod%d" % t, align_bytes=64) for t in range(PACK)]
+        for t in range(PACK):
+            nc.vector.tensor_tensor(prod[t][:], yw[t][:].indirect(l3[:]), g1[t][:], ALU.mult)
+        zq = keep.tile([P, N], U32, name="zq", align_bytes=64)
+        zsc = keep.tile([P, N], U8, name="zsc", align_bytes=64)
+        zb = []
+        for h in range(2):
+            cols = slice(h * HALF, (h + 1) * HALF)
+            z4 = keep.tile([P, PACK, HALF], F32, name="z4_%d" % h, tag=("g1_3", "yw3")[h])
+            for t in range(PACK):
+                nc.vector.tensor_tensor(z4[:, t, :], tgw[t][:].indirect(l2[:, h * 16:(h + 1) * 16]), prod[t][:, cols], ALU.add)
+            zb.append(keep.tile([P, PACK * HALF], BF16, name="zb%d" % h, align_bytes=64))
+            nc.scalar.copy(zb[h][:].rearrange("p (c i t) -> p c t i", i=4, t=PACK),
+                           z4[:].rearrange("p t (c i) -> p c t i", i=4))
+        xc_w = keep.tile([P, N], U32, name="xc_w", tag="prod%d" % (PACK - 2), align_bytes=64)
+        nc.vector.tensor_copy(xc_w[:].rearrange("p (t a b) -> p a t b", t=PACK, b=8), xw[:].indirect(lcand[:]))
+        for h in range(2):
+            cols = slice(h * HALF, (h + 1) * HALF)
+            nc.vector.quantize_mx(out=zq[:, cols].bitcast(FP8X4), scales=zsc[:, cols], in_=zb[h][:])
+
+        out_rows = out.rearrange("(a t b) j -> t a b j", t=PACK, b=8)
+        mw = [keep.tile([P, WIN], F32, name="mw%d" % t) for t in range(PACK)]
+        mp = [keep.tile([P, N], F32, name="mp%d" % t) for t in range(PACK)]
+        for t in range(PACK):
+            cols = slice(t * P, (t + 1) * P)
+            acc = psum.tile([P, N], F32, name="sacc%d" % t)
+            nc.tensor.matmul_mx(out=acc[:], lhsT=xc_w[:, cols].bitcast(FP8X4), lhsT_scale=xc_s[:, cols],
+                                rhs=zq[:].bitcast(FP8X4), rhs_scale=zsc[:], start=True, stop=True)
+            nc.scalar.activation(mw[t][:, :N], acc[:], COPY, scale=0.0625)
+            nc.scalar.activation(mp[t][:], acc[:], COPY, scale=0.0625)
+
+        u = [keep.tile([P, N], F32, name="u%d" % t) for t in range(PACK)]
+        v = [keep.tile([P, N], F32, name="v%d" % t) for t in range(PACK)]
+        w = [keep.tile([P, N], F32, name="w%d" % t) for t in range(PACK)]
+        res = [keep.tile([P, N], F32, name="res%d" % t) for t in range(PACK)]
+
+        def step_u(t):
+            nc.vector.tensor_tensor(u[t][:], mw[t][:].indirect(l5[:]), mp[t][:], ALU.subtract)
+
+        def step_v(t):
+            nc.vector.tensor_tensor(v[t][:], mw[t][:].indirect(l6[:]), mp[t][:], ALU.subtract)
+
+        def step_w(t):
+            nc.vector.tensor_tensor(w[t][:], u[t][:], v[t][:], ALU.max)
+
+        def step_out(t, pieces):
+            width = N // pieces
+            for h in range(pieces):
+                cols = slice(h * width, (h + 1) * width)
+                nc.vector.tensor_tensor(res[t][:, cols], mw[t][:].indirect(l4[:, h * width // 16:(h + 1) * width // 16]),
+                                        w[t][:, cols], ALU.subtract)
+                nc.sync.dma_start(out_rows[t][:, :, cols], res[t][:, cols])
+
+        step_u(0)
+        step_v(0)
+        for t in range(1, PACK):
+            step_u(t)
+            step_w(t - 1)
+            step_v(t)
+            if t < PACK - 1:
+                step_out(t - 1, 1)
+        step_w(PACK - 1)
+        step_out(PACK - 2, 1)
+        step_out(PACK - 1, 2)

@@ -1,6 +1,7 @@
 from contextlib import ExitStack
 
 import concourse.mybir as mybir
+from concourse.masks import make_identity
 
 F32 = mybir.dt.float32
 BF16 = mybir.dt.bfloat16
@@ -11,6 +12,7 @@ U8 = mybir.dt.uint8
 FP8X4 = mybir.dt.float8_e4m3fn_x4
 ALU = mybir.AluOpType
 COPY = mybir.ActivationFunctionType.Copy
+RELU = mybir.ActivationFunctionType.Relu
 
 P = 128
 T = 2048
@@ -36,23 +38,30 @@ def tile_picked_candkindatrim_none_p_kernel(tc, x_words, x_scales, w1, tab, gs, 
         xs = keep.tile([P, T], U8, name="xs", align_bytes=64)
         nc.vector.memset(xs[:].bitcast(I32), 0)
 
+        ident = keep.tile([P, P], F32, name="ident")
+        make_identity(nc, ident[:])
         tab_rows = tab.rearrange("(p t) c -> p t c", t=PACK)
         tabw = [keep.tile([P, WIN], F32, name="tabw%d" % t) for t in range(PACK)]
-        l1 = load_list(n1, "l1")
-        gs_t = keep.tile([P, PACK], F32, name="gs_t")
-        for t in range(PACK):
+
+        def load_tab(t):
             nc.sync.dma_start(tabw[t][:, :N], tab_rows[:, t, :])
-            if t == 0:
-                nc.sync.dma_start(gs_t[:], gs.rearrange("(p t) o -> p (t o)", t=PACK))
+
+        load_tab(0)
+        l1 = load_list(n1, "l1")
+        load_tab(1)
+        for q in range(4):
+            nc.sync.dma_start(xs[32 * q:32 * q + 4, :].bitcast(I32), x_scales[0, 4 * q:4 * q + 4, :].bitcast(I32))
         w_rows = w1.rearrange("(p j) c -> p j c", j=PACK)
         wraw = [keep.tile([P, PACK, HALF], F32, name="wraw%d" % h) for h in range(2)]
         for h in range(2):
             nc.sync.dma_start(wraw[h][:], w_rows[:, :, h * HALF:(h + 1) * HALF])
-        for q in range(4):
-            nc.scalar.dma_start(xs[32 * q:32 * q + 4, :].bitcast(I32), x_scales[0, 4 * q:4 * q + 4, :].bitcast(I32))
         loffs = load_list(offs, "loffs")
+        load_tab(2)
+        gs_t = keep.tile([P, PACK], F32, name="gs_t")
+        nc.sync.dma_start(gs_t[:], gs.rearrange("(p t) o -> p (t o)", t=PACK))
         xw = keep.tile([P, T], U32, name="xw", align_bytes=64)
         nc.sync.dma_start(xw[:].bitcast(I32), x_words[0].rearrange("p c r -> p (c r)").bitcast(I32))
+        load_tab(3)
         lcand = load_list(cand, "lcand")
         l3 = load_list(n3, "l3")
         l2 = load_list(n2, "l2")
@@ -84,7 +93,7 @@ def tile_picked_candkindatrim_none_p_kernel(tc, x_words, x_scales, w1, tab, gs, 
         yw = [keep.tile([P, WIN], F32, name="yw%d" % t, tag="yw%d" % t) for t in range(PACK)]
         for t in range(PACK):
             cols = slice(t * P, (t + 1) * P)
-            acc = psum.tile([P, N], F32, name="yacc%d" % t)
+            acc = psum.tile([P, N], F32, name="yacc%d" % t, tag="bank%d" % t)
             nc.tensor.matmul_mx(out=acc[:], lhsT=wq[:, cols].bitcast(FP8X4), lhsT_scale=wsc[:, cols],
                                 rhs=xq_w[:].bitcast(FP8X4), rhs_scale=xq_s[:], start=True, stop=True)
             nc.scalar.activation(yw[t][:, :N], acc[:], COPY, scale=gs_t[:, t:t + 1])
@@ -95,8 +104,8 @@ def tile_picked_candkindatrim_none_p_kernel(tc, x_words, x_scales, w1, tab, gs, 
         prod = [keep.tile([P, N], F32, name="prod%d" % t, tag="prod%d" % t, align_bytes=64) for t in range(PACK)]
         for t in range(PACK):
             nc.vector.tensor_tensor(prod[t][:], yw[t][:].indirect(l3[:]), g1[t][:], ALU.mult)
-        zq = keep.tile([P, N], U32, name="zq", align_bytes=64)
-        zsc = keep.tile([P, N], U8, name="zsc", align_bytes=64)
+        zq = [keep.tile([P, HALF], U32, name="zq%d" % h, align_bytes=64) for h in range(2)]
+        zsc = [keep.tile([P, HALF], U8, name="zsc%d" % h, align_bytes=64) for h in range(2)]
         zb = []
         for h in range(2):
             cols = slice(h * HALF, (h + 1) * HALF)
@@ -109,50 +118,81 @@ def tile_picked_candkindatrim_none_p_kernel(tc, x_words, x_scales, w1, tab, gs, 
         xc_w = keep.tile([P, N], U32, name="xc_w", tag="prod%d" % (PACK - 2), align_bytes=64)
         nc.vector.tensor_copy(xc_w[:].rearrange("p (t a b) -> p a t b", t=PACK, b=8), xw[:].indirect(lcand[:]))
         for h in range(2):
-            cols = slice(h * HALF, (h + 1) * HALF)
-            nc.vector.quantize_mx(out=zq[:, cols].bitcast(FP8X4), scales=zsc[:, cols], in_=zb[h][:])
+            nc.vector.quantize_mx(out=zq[h][:].bitcast(FP8X4), scales=zsc[h][:], in_=zb[h][:])
 
         out_rows = out.rearrange("(a t b) j -> t a b j", t=PACK, b=8)
-        mw = [keep.tile([P, WIN], F32, name="mw%d" % t) for t in range(PACK)]
-        mp = [keep.tile([P, N], F32, name="mp%d" % t) for t in range(PACK)]
-        for t in range(PACK):
-            cols = slice(t * P, (t + 1) * P)
-            acc = psum.tile([P, N], F32, name="sacc%d" % t)
-            nc.tensor.matmul_mx(out=acc[:], lhsT=xc_w[:, cols].bitcast(FP8X4), lhsT_scale=xc_s[:, cols],
-                                rhs=zq[:].bitcast(FP8X4), rhs_scale=zsc[:], start=True, stop=True)
-            nc.scalar.activation(mw[t][:, :N], acc[:], COPY, scale=0.0625)
-            nc.scalar.activation(mp[t][:], acc[:], COPY, scale=0.0625)
+        last = PACK - 1
+        sw = [keep.tile([P, WIN], F32, name="sw%d" % t) for t in range(PACK)]
+        plain = keep.tile([P, N], F32, name="plain")
+        halves = [(slice(h * HALF, (h + 1) * HALF), slice(h * 16, (h + 1) * 16)) for h in range(2)]
 
-        u = [keep.tile([P, N], F32, name="u%d" % t) for t in range(PACK)]
-        v = [keep.tile([P, N], F32, name="v%d" % t) for t in range(PACK)]
-        w = [keep.tile([P, N], F32, name="w%d" % t) for t in range(PACK)]
+        def score(acc, t, h):
+            rows = slice(t * P, (t + 1) * P)
+            nc.tensor.matmul_mx(out=acc, lhsT=xc_w[:, rows].bitcast(FP8X4), lhsT_scale=xc_s[:, rows],
+                                rhs=zq[h][:].bitcast(FP8X4), rhs_scale=zsc[h][:], start=True, stop=True)
+
+        for h in range(2):
+            acc = psum.tile([P, HALF], F32, name="sacc0_%d" % h, tag="bank%d" % (4 * h))
+            score(acc[:], 0, h)
+            nc.scalar.activation(sw[0][:, halves[h][0]], acc[:], COPY, scale=-0.0625)
+        for t in range(1, PACK):
+            acc = psum.tile([P, N], F32, name="sacc%d" % t, tag="bank%d" % t)
+            for h in (1, 0):
+                score(acc[:, halves[h][0]], t, h)
+            nc.scalar.activation(sw[t][:, :N], acc[:], COPY, scale=0.0625 if t == last else -0.0625)
+            if t == last:
+                nc.scalar.activation(plain[:], acc[:], COPY, scale=0.0625)
+
+        g5 = [keep.tile([P, N], F32, name="g5_%d" % t) for t in range(last)]
         res = [keep.tile([P, N], F32, name="res%d" % t) for t in range(PACK)]
 
-        def step_u(t):
-            nc.vector.tensor_tensor(u[t][:], mw[t][:].indirect(l5[:]), mp[t][:], ALU.subtract)
+        def fetch5(t):
+            nc.vector.tensor_copy(g5[t][:], sw[t][:].indirect(l5[:]))
 
-        def step_v(t):
-            nc.vector.tensor_tensor(v[t][:], mw[t][:].indirect(l6[:]), mp[t][:], ALU.subtract)
-
-        def step_w(t):
-            nc.vector.tensor_tensor(w[t][:], u[t][:], v[t][:], ALU.max)
-
-        def step_out(t, pieces):
+        def finish_by_transposes(t):
+            d = keep.tile([P, N], F32, name="d%d" % t)
+            nc.vector.tensor_tensor(d[:], sw[t][:].indirect(l6[:]), g5[t][:], ALU.subtract)
+            r = keep.tile([P, N], F32, name="r%d" % t, tag="h%d" % (t - 1))
+            nc.scalar.activation(r[:], d[:], RELU, scale=-1.0)
+            hh = keep.tile([P, N], F32, name="h%d" % t, tag="h%d" % t)
+            nc.vector.tensor_tensor(hh[:], sw[t][:].indirect(l4[:]), g5[t][:], ALU.subtract)
+            terms = (sw[t], r, hh) if t == last - 1 else (r, sw[t], hh)
+            pieces = 2 if t == last - 1 else 1
             width = N // pieces
-            for h in range(pieces):
-                cols = slice(h * width, (h + 1) * width)
-                nc.vector.tensor_tensor(res[t][:, cols], mw[t][:].indirect(l4[:, h * width // 16:(h + 1) * width // 16]),
-                                        w[t][:, cols], ALU.subtract)
-                nc.sync.dma_start(out_rows[t][:, :, cols], res[t][:, cols])
+            blocks = width // P
+            turned = [psum.tile([P, width], F32, name="turned%d_%d" % (t, k), tag="bank%d" % (5 + (t + k) % 2))
+                      for k in range(pieces)]
+            for i, term in enumerate(terms):
+                for b in range(N // P):
+                    k, c = divmod(b, blocks)
+                    nc.tensor.matmul(turned[k][:, c * P:(c + 1) * P], term[:, b * P:(b + 1) * P], ident[:], is_transpose=True,
+                                     start=(i == 0 and c == 0), stop=(i == len(terms) - 1 and c == blocks - 1))
+            total = keep.tile([P, N], F32, name="total%d" % t)
+            for k in range(pieces):
+                cols = slice(k * width, (k + 1) * width)
+                nc.scalar.copy(total[:, cols], turned[k][:])
+            for k in range(pieces):
+                cols = slice(k * width, (k + 1) * width)
+                back = psum.tile([P, width], F32, name="back%d_%d" % (t, k), tag="bank%d" % (7 * (1 - k)))
+                for c in range(blocks):
+                    nc.tensor.transpose(back[:, c * P:(c + 1) * P], total[:, k * width + c * P:k * width + (c + 1) * P], ident[:])
+                nc.scalar.activation(res[t][:, cols], back[:], COPY, scale=-1.0)
+                nc.scalar.dma_start(out_rows[t][:, :, cols], res[t][:, cols])
 
-        step_u(0)
-        step_v(0)
-        for t in range(1, PACK):
-            step_u(t)
-            step_w(t - 1)
-            step_v(t)
-            if t < PACK - 1:
-                step_out(t - 1, 1)
-        step_w(PACK - 1)
-        step_out(PACK - 2, 1)
-        step_out(PACK - 1, 2)
+        fetch5(0)
+        for t in range(last):
+            if t + 1 < last:
+                fetch5(t + 1)
+            finish_by_transposes(t)
+
+        u = keep.tile([P, N], F32, name="u")
+        v = keep.tile([P, N], F32, name="v")
+        w = keep.tile([P, N], F32, name="w")
+        nc.vector.tensor_tensor(u[:], sw[last][:].indirect(l5[:]), plain[:], ALU.subtract)
+        for cols, lcols in halves:
+            nc.vector.tensor_tensor(v[:, cols], sw[last][:].indirect(l6[:, lcols]), plain[:, cols], ALU.subtract)
+        for cols, lcols in halves:
+            nc.vector.tensor_tensor(w[:, cols], u[:, cols], v[:, cols], ALU.max)
+        for cols, lcols in halves:
+            nc.vector.tensor_tensor(res[last][:, cols], sw[last][:].indirect(l4[:, lcols]), w[:, cols], ALU.subtract)
+            nc.sync.dma_start(out_rows[last][:, :, cols], res[last][:, cols])

@@ -49,20 +49,20 @@ def tile_picked_candkindatrim_none_p_kernel(tc, x_words, x_scales, w1, tab, gs, 
         load_tab(0)
         l1 = load_list(n1, "l1")
         load_tab(1)
-        for q in range(4):
-            nc.sync.dma_start(xs[32 * q:32 * q + 4, :].bitcast(I32), x_scales[0, 4 * q:4 * q + 4, :].bitcast(I32))
         w_rows = w1.rearrange("(p j) c -> p j c", j=PACK)
         wraw = [keep.tile([P, PACK, HALF], F32, name="wraw%d" % h) for h in range(2)]
-        for h in range(2):
-            nc.sync.dma_start(wraw[h][:], w_rows[:, :, h * HALF:(h + 1) * HALF])
+        nc.sync.dma_start(wraw[0][:], w_rows[:, :, :HALF])
+        for q in (0, 2, 1, 3):
+            nc.sync.dma_start(xs[32 * q:32 * q + 4, :].bitcast(I32), x_scales[0, 4 * q:4 * q + 4, :].bitcast(I32))
         loffs = load_list(offs, "loffs")
-        load_tab(2)
-        gs_t = keep.tile([P, PACK], F32, name="gs_t")
-        nc.sync.dma_start(gs_t[:], gs.rearrange("(p t) o -> p (t o)", t=PACK))
+        nc.sync.dma_start(wraw[1][:], w_rows[:, :, HALF:])
+        lcand = load_list(cand, "lcand")
         xw = keep.tile([P, T], U32, name="xw", align_bytes=64)
         nc.sync.dma_start(xw[:].bitcast(I32), x_words[0].rearrange("p c r -> p (c r)").bitcast(I32))
+        gs_t = keep.tile([P, PACK], F32, name="gs_t")
+        nc.sync.dma_start(gs_t[:], gs.rearrange("(p t) o -> p (t o)", t=PACK))
+        load_tab(2)
         load_tab(3)
-        lcand = load_list(cand, "lcand")
         l3 = load_list(n3, "l3")
         l2 = load_list(n2, "l2")
         l4 = load_list(n4, "l4")
@@ -156,11 +156,11 @@ def tile_picked_candkindatrim_none_p_kernel(tc, x_words, x_scales, w1, tab, gs, 
             nc.scalar.activation(r[:], d[:], RELU, scale=-1.0)
             hh = keep.tile([P, N], F32, name="h%d" % t, tag="h%d" % t)
             nc.vector.tensor_tensor(hh[:], sw[t][:].indirect(l4[:]), g5[t][:], ALU.subtract)
-            terms = (sw[t], r, hh) if t == last - 1 else (r, sw[t], hh)
+            terms = (sw[t], r, hh)
             pieces = 2 if t == last - 1 else 1
             width = N // pieces
             blocks = width // P
-            turned = [psum.tile([P, width], F32, name="turned%d_%d" % (t, k), tag="bank%d" % (5 + (t + k) % 2))
+            turned = [psum.tile([P, width], F32, name="turned%d_%d" % (t, k), tag="bank%d" % (2 + t if pieces == 1 else 5 + k))
                       for k in range(pieces)]
             for i, term in enumerate(terms):
                 for b in range(N // P):

@@ -38,10 +38,12 @@ def tile_picked_candkindatrim_none_p_kernel(tc, x_words, x_scales, w1, tab, gs, 
         xs = keep.tile([P, T], U8, name="xs", align_bytes=64)
         nc.vector.memset(xs[:].bitcast(I32), 0)
 
+        factor = keep.tile([P, 8], F32, name="factor", tag="pair0")
+        nc.gpsimd.memset(factor[:, 0:1], -0.0625)
         ident = keep.tile([P, P], F32, name="ident")
         make_identity(nc, ident[:])
         tab_rows = tab.rearrange("(p t) c -> p t c", t=PACK)
-        tabw = [keep.tile([P, WIN], F32, name="tabw%d" % t) for t in range(PACK)]
+        tabw = [keep.tile([P, WIN], F32, name="tabw%d" % t, tag="tabw%d" % t) for t in range(PACK)]
 
         def load_tab(t):
             nc.sync.dma_start(tabw[t][:, :N], tab_rows[:, t, :])
@@ -73,20 +75,20 @@ def tile_picked_candkindatrim_none_p_kernel(tc, x_words, x_scales, w1, tab, gs, 
         for t in range(PACK):
             nc.vector.tensor_copy(g1[t][:], tabw[t][:].indirect(l1[:]))
 
-        wb = keep.tile([P, PACK * N], BF16, name="wb", align_bytes=64)
+        wb = keep.tile([P, PACK * N], BF16, name="wb", tag="wb", align_bytes=64)
         wb_v = wb[:].rearrange("p (t m j) -> p m j t", t=PACK, j=PACK)
         for h in range(2):
             nc.scalar.copy(wb_v[:, h * 64:(h + 1) * 64], wraw[h][:].rearrange("p j (m t) -> p m j t", t=PACK))
-        xq_s = keep.tile([P, N], U8, name="xq_s", align_bytes=64)
+        xq_s = keep.tile([P, N], U8, name="xq_s", tag="xq_s", align_bytes=64)
         nc.vector.tensor_copy(xq_s[:], xs[:].indirect(loffs[:]))
-        wq = keep.tile([P, N], U32, name="wq", align_bytes=64)
-        wsc = keep.tile([P, N], U8, name="wsc", align_bytes=64)
+        wq = keep.tile([P, N], U32, name="wq", tag="wq", align_bytes=64)
+        wsc = keep.tile([P, N], U8, name="wsc", tag="wsc", align_bytes=64)
         nc.vector.quantize_mx(out=wq[:].bitcast(FP8X4), scales=wsc[:], in_=wb[:])
-        xq_w = keep.tile([P, N], U32, name="xq_w", align_bytes=64)
+        xq_w = keep.tile([P, N], U32, name="xq_w", tag="xq_w", align_bytes=64)
         nc.vector.tensor_copy(xq_w[:], xw[:].indirect(loffs[:]))
         xc_s0 = keep.tile([P, N], U8, name="xc_s0", align_bytes=64)
         nc.vector.tensor_copy(xc_s0[:], xs[:].indirect(lcand[:]))
-        xc_s = keep.tile([P, N], U8, name="xc_s", align_bytes=64)
+        xc_s = keep.tile([P, N], U8, name="xc_s", tag="wb", align_bytes=64)
         nc.vector.tensor_copy(xc_s[:].bitcast(I32).rearrange("p (t a w) -> p t a w", t=PACK, w=2),
                               xc_s0[:].bitcast(I32).rearrange("p (a t w) -> p t a w", t=PACK, w=2))
 
@@ -97,19 +99,19 @@ def tile_picked_candkindatrim_none_p_kernel(tc, x_words, x_scales, w1, tab, gs, 
             nc.tensor.matmul_mx(out=acc[:], lhsT=wq[:, cols].bitcast(FP8X4), lhsT_scale=wsc[:, cols],
                                 rhs=xq_w[:].bitcast(FP8X4), rhs_scale=xq_s[:], start=True, stop=True)
             nc.scalar.activation(yw[t][:, :N], acc[:], COPY, scale=gs_t[:, t:t + 1])
-        tgw = [keep.tile([P, WIN], F32, name="tgw%d" % t) for t in range(PACK)]
+        tgw = [keep.tile([P, WIN], F32, name="tgw%d" % t, tag=("wq", "wsc", "xq_w", "xq_s")[t], align_bytes=64) for t in range(PACK)]
         for t in range(PACK):
             nc.scalar.activation(tgw[t][:, :N], tabw[t][:, :N], COPY, scale=gs_t[:, t:t + 1])
 
         prod = [keep.tile([P, N], F32, name="prod%d" % t, tag="prod%d" % t, align_bytes=64) for t in range(PACK)]
         for t in range(PACK):
             nc.vector.tensor_tensor(prod[t][:], yw[t][:].indirect(l3[:]), g1[t][:], ALU.mult)
-        zq = [keep.tile([P, HALF], U32, name="zq%d" % h, align_bytes=64) for h in range(2)]
+        zq = [keep.tile([P, HALF], U32, name="zq%d" % h, tag="zq%d" % h, align_bytes=64) for h in range(2)]
         zsc = [keep.tile([P, HALF], U8, name="zsc%d" % h, align_bytes=64) for h in range(2)]
         zb = []
         for h in range(2):
             cols = slice(h * HALF, (h + 1) * HALF)
-            z4 = keep.tile([P, PACK, HALF], F32, name="z4_%d" % h, tag=("g1_3", "yw3")[h])
+            z4 = keep.tile([P, PACK, HALF], F32, name="z4_%d" % h, tag=("z4_0", "tabw3")[h])
             for t in range(PACK):
                 nc.vector.tensor_tensor(z4[:, t, :], tgw[t][:].indirect(l2[:, h * 16:(h + 1) * 16]), prod[t][:, cols], ALU.add)
             zb.append(keep.tile([P, PACK * HALF], BF16, name="zb%d" % h, align_bytes=64))
@@ -139,7 +141,8 @@ def tile_picked_candkindatrim_none_p_kernel(tc, x_words, x_scales, w1, tab, gs, 
             acc = psum.tile([P, N], F32, name="sacc%d" % t, tag="bank%d" % t)
             for h in (1, 0):
                 score(acc[:, halves[h][0]], t, h)
-            nc.scalar.activation(sw[t][:, :N], acc[:], COPY, scale=0.0625 if t == last else -0.0625)
+            scale = factor[:, 0:1] if t == 1 else 0.0625 if t == last else -0.0625
+            nc.scalar.activation(sw[t][:, :N], acc[:], COPY, scale=scale)
             if t == last:
                 nc.scalar.activation(plain[:], acc[:], COPY, scale=0.0625)
 
@@ -150,12 +153,12 @@ def tile_picked_candkindatrim_none_p_kernel(tc, x_words, x_scales, w1, tab, gs, 
             nc.vector.tensor_copy(g5[t][:], sw[t][:].indirect(l5[:]))
 
         def finish_by_transposes(t):
-            d = keep.tile([P, N], F32, name="d%d" % t)
-            nc.vector.tensor_tensor(d[:], sw[t][:].indirect(l6[:]), g5[t][:], ALU.subtract)
-            r = keep.tile([P, N], F32, name="r%d" % t, tag="h%d" % (t - 1))
-            nc.scalar.activation(r[:], d[:], RELU, scale=-1.0)
-            hh = keep.tile([P, N], F32, name="h%d" % t, tag="h%d" % t)
-            nc.vector.tensor_tensor(hh[:], sw[t][:].indirect(l4[:]), g5[t][:], ALU.subtract)
+            pair = keep.tile([P, 2 * N], F32, name="pair%d" % t, tag="pair%d" % t)
+            d, hh = pair[:, :N], pair[:, N:]
+            nc.vector.tensor_tensor(d, sw[t][:].indirect(l6[:]), g5[t][:], ALU.subtract)
+            r = keep.tile([P, N], F32, name="r%d" % t, tag="pair%d" % (t - 1))
+            nc.scalar.activation(r[:], d, RELU, scale=-1.0)
+            nc.vector.tensor_tensor(hh, sw[t][:].indirect(l4[:]), g5[t][:], ALU.subtract)
             terms = (sw[t], r, hh)
             pieces = 2 if t == last - 1 else 1
             width = N // pieces

from contextlib import ExitStack

import concourse.mybir as mybir
from concourse.masks import make_identity

F32 = mybir.dt.float32
BF16 = mybir.dt.bfloat16
I32 = mybir.dt.int32
U32 = mybir.dt.uint32
U16 = mybir.dt.uint16
U8 = mybir.dt.uint8
FP8X4 = mybir.dt.float8_e4m3fn_x4
ALU = mybir.AluOpType
COPY = mybir.ActivationFunctionType.Copy
RELU = mybir.ActivationFunctionType.Relu

P = 128
T = 2048
N = 512
PACK = 4
WIN = 2 * N
HALF = N // 2
FLOPS = 2 * 2 * 512 * 512 * 512


def tile_picked_candkindatrim_none_p_kernel(tc, x_words, x_scales, w1, tab, gs, offs, n1, n2, n3, cand, n4, n5, n6, out):
    nc = tc.nc
    with ExitStack() as ctx:
        lists = ctx.enter_context(tc.tile_pool(name="lists", bufs=1))
        keep = ctx.enter_context(tc.tile_pool(name="keep", bufs=1))
        psum = ctx.enter_context(tc.psum_pool(name="psum", bufs=1))

        def load_list(src, name):
            tile = lists.tile([P, N // 16], U16, name=name)
            nc.sync.dma_start(tile[:], src)
            return tile

        xs = keep.tile([P, T], U8, name="xs", align_bytes=64)
        nc.vector.memset(xs[:].bitcast(I32), 0)

        factor = keep.tile([P, 8], F32, name="factor", tag="pair0")
        nc.gpsimd.memset(factor[:, 0:1], -0.0625)
        ident = keep.tile([P, P], F32, name="ident")
        make_identity(nc, ident[:])
        tab_rows = tab.rearrange("(p t) c -> p t c", t=PACK)
        tabw = [keep.tile([P, WIN], F32, name="tabw%d" % t, tag="tabw%d" % t) for t in range(PACK)]

        def load_tab(t):
            nc.sync.dma_start(tabw[t][:, :N], tab_rows[:, t, :])

        load_tab(0)
        l1 = load_list(n1, "l1")
        load_tab(1)
        w_rows = w1.rearrange("(p j) c -> p j c", j=PACK)
        wraw = [keep.tile([P, PACK, HALF], F32, name="wraw%d" % h) for h in range(2)]
        nc.sync.dma_start(wraw[0][:], w_rows[:, :, :HALF])
        for q in (0, 2, 1, 3):
            nc.sync.dma_start(xs[32 * q:32 * q + 4, :].bitcast(I32), x_scales[0, 4 * q:4 * q + 4, :].bitcast(I32))
        loffs = load_list(offs, "loffs")
        nc.sync.dma_start(wraw[1][:], w_rows[:, :, HALF:])
        lcand = load_list(cand, "lcand")
        xw = keep.tile([P, T], U32, name="xw", align_bytes=64)
        nc.sync.dma_start(xw[:].bitcast(I32), x_words[0].rearrange("p c r -> p (c r)").bitcast(I32))
        gs_t = keep.tile([P, PACK], F32, name="gs_t")
        nc.sync.dma_start(gs_t[:], gs.rearrange("(p t) o -> p (t o)", t=PACK))
        load_tab(2)
        load_tab(3)
        l3 = load_list(n3, "l3")
        l2 = load_list(n2, "l2")
        l4 = load_list(n4, "l4")
        l5 = load_list(n5, "l5")
        l6 = load_list(n6, "l6")

        g1 = [keep.tile([P, N], F32, name="g1_%d" % t, tag="g1_%d" % t) for t in range(PACK)]
        for t in range(PACK):
            nc.vector.tensor_copy(g1[t][:], tabw[t][:].indirect(l1[:]))

        wb = keep.tile([P, PACK * N], BF16, name="wb", tag="wb", align_bytes=64)
        wb_v = wb[:].rearrange("p (t m j) -> p m j t", t=PACK, j=PACK)
        for h in range(2):
            nc.scalar.copy(wb_v[:, h * 64:(h + 1) * 64], wraw[h][:].rearrange("p j (m t) -> p m j t", t=PACK))
        xq_s = keep.tile([P, N], U8, name="xq_s", tag="xq_s", align_bytes=64)
        nc.vector.tensor_copy(xq_s[:], xs[:].indirect(loffs[:]))
        wq = keep.tile([P, N], U32, name="wq", tag="wq", align_bytes=64)
        wsc = keep.tile([P, N], U8, name="wsc", tag="wsc", align_bytes=64)
        nc.vector.quantize_mx(out=wq[:].bitcast(FP8X4), scales=wsc[:], in_=wb[:])
        xq_w = keep.tile([P, N], U32, name="xq_w", tag="xq_w", align_bytes=64)
        nc.vector.tensor_copy(xq_w[:], xw[:].indirect(loffs[:]))
        xc_s0 = keep.tile([P, N], U8, name="xc_s0", align_bytes=64)
        nc.vector.tensor_copy(xc_s0[:], xs[:].indirect(lcand[:]))
        xc_s = keep.tile([P, N], U8, name="xc_s", tag="wb", align_bytes=64)
        nc.vector.tensor_copy(xc_s[:].bitcast(I32).rearrange("p (t a w) -> p t a w", t=PACK, w=2),
                              xc_s0[:].bitcast(I32).rearrange("p (a t w) -> p t a w", t=PACK, w=2))

        yw = [keep.tile([P, WIN], F32, name="yw%d" % t, tag="yw%d" % t) for t in range(PACK)]
        for t in range(PACK):
            cols = slice(t * P, (t + 1) * P)
            acc = psum.tile([P, N], F32, name="yacc%d" % t, tag="bank%d" % t)
            nc.tensor.matmul_mx(out=acc[:], lhsT=wq[:, cols].bitcast(FP8X4), lhsT_scale=wsc[:, cols],
                                rhs=xq_w[:].bitcast(FP8X4), rhs_scale=xq_s[:], start=True, stop=True)
            nc.scalar.activation(yw[t][:, :N], acc[:], COPY, scale=gs_t[:, t:t + 1])
        tgw = [keep.tile([P, WIN], F32, name="tgw%d" % t, tag=("wq", "wsc", "xq_w", "xq_s")[t], align_bytes=64) for t in range(PACK)]
        for t in range(PACK):
            nc.scalar.activation(tgw[t][:, :N], tabw[t][:, :N], COPY, scale=gs_t[:, t:t + 1])

        prod = [keep.tile([P, N], F32, name="prod%d" % t, tag="prod%d" % t, align_bytes=64) for t in range(PACK)]
        for t in range(PACK):
            nc.vector.tensor_tensor(prod[t][:], yw[t][:].indirect(l3[:]), g1[t][:], ALU.mult)
        zq = [keep.tile([P, HALF], U32, name="zq%d" % h, tag="zq%d" % h, align_bytes=64) for h in range(2)]
        zsc = [keep.tile([P, HALF], U8, name="zsc%d" % h, align_bytes=64) for h in range(2)]
        zb = []
        for h in range(2):
            cols = slice(h * HALF, (h + 1) * HALF)
            z4 = keep.tile([P, PACK, HALF], F32, name="z4_%d" % h, tag=("z4_0", "tabw3")[h])
            for t in range(PACK):
                nc.vector.tensor_tensor(z4[:, t, :], tgw[t][:].indirect(l2[:, h * 16:(h + 1) * 16]), prod[t][:, cols], ALU.add)
            zb.append(keep.tile([P, PACK * HALF], BF16, name="zb%d" % h, align_bytes=64))
            nc.scalar.copy(zb[h][:].rearrange("p (c i t) -> p c t i", i=4, t=PACK),
                           z4[:].rearrange("p t (c i) -> p c t i", i=4))
        xc_w = keep.tile([P, N], U32, name="xc_w", tag="prod%d" % (PACK - 2), align_bytes=64)
        nc.vector.tensor_copy(xc_w[:].rearrange("p (t a b) -> p a t b", t=PACK, b=8), xw[:].indirect(lcand[:]))
        for h in range(2):
            nc.vector.quantize_mx(out=zq[h][:].bitcast(FP8X4), scales=zsc[h][:], in_=zb[h][:])

        out_rows = out.rearrange("(a t b) j -> t a b j", t=PACK, b=8)
        last = PACK - 1
        sw = [keep.tile([P, WIN], F32, name="sw%d" % t) for t in range(PACK)]
        plain = keep.tile([P, N], F32, name="plain")
        halves = [(slice(h * HALF, (h + 1) * HALF), slice(h * 16, (h + 1) * 16)) for h in range(2)]

        def score(acc, t, h):
            rows = slice(t * P, (t + 1) * P)
            nc.tensor.matmul_mx(out=acc, lhsT=xc_w[:, rows].bitcast(FP8X4), lhsT_scale=xc_s[:, rows],
                                rhs=zq[h][:].bitcast(FP8X4), rhs_scale=zsc[h][:], start=True, stop=True)

        for h in range(2):
            acc = psum.tile([P, HALF], F32, name="sacc0_%d" % h, tag="bank%d" % (4 * h))
            score(acc[:], 0, h)
            nc.scalar.activation(sw[0][:, halves[h][0]], acc[:], COPY, scale=-0.0625)
        for t in range(1, PACK):
            acc = psum.tile([P, N], F32, name="sacc%d" % t, tag="bank%d" % t)
            for h in (1, 0):
                score(acc[:, halves[h][0]], t, h)
            scale = factor[:, 0:1] if t == 1 else 0.0625 if t == last else -0.0625
            nc.scalar.activation(sw[t][:, :N], acc[:], COPY, scale=scale)
            if t == last:
                nc.scalar.activation(plain[:], acc[:], COPY, scale=0.0625)

        g5 = [keep.tile([P, N], F32, name="g5_%d" % t) for t in range(last)]
        res = [keep.tile([P, N], F32, name="res%d" % t) for t in range(PACK)]

        def fetch5(t):
            nc.vector.tensor_copy(g5[t][:], sw[t][:].indirect(l5[:]))

        def finish_by_transposes(t):
            pair = keep.tile([P, 2 * N], F32, name="pair%d" % t, tag="pair%d" % t)
            d, hh = pair[:, :N], pair[:, N:]
            nc.vector.tensor_tensor(d, sw[t][:].indirect(l6[:]), g5[t][:], ALU.subtract)
            r = keep.tile([P, N], F32, name="r%d" % t, tag="pair%d" % (t - 1))
            nc.scalar.activation(r[:], d, RELU, scale=-1.0)
            nc.vector.tensor_tensor(hh, sw[t][:].indirect(l4[:]), g5[t][:], ALU.subtract)
            terms = (sw[t], r, hh)
            pieces = 2 if t == last - 1 else 1
            width = N // pieces
            blocks = width // P
            turned = [psum.tile([P, width], F32, name="turned%d_%d" % (t, k), tag="bank%d" % (2 + t if pieces == 1 else 5 + k))
                      for k in range(pieces)]
            for i, term in enumerate(terms):
                for b in range(N // P):
                    k, c = divmod(b, blocks)
                    nc.tensor.matmul(turned[k][:, c * P:(c + 1) * P], term[:, b * P:(b + 1) * P], ident[:], is_transpose=True,
                                     start=(i == 0 and c == 0), stop=(i == len(terms) - 1 and c == blocks - 1))
            total = keep.tile([P, N], F32, name="total%d" % t)
            for k in range(pieces):
                cols = slice(k * width, (k + 1) * width)
                nc.scalar.copy(total[:, cols], turned[k][:])
            for k in range(pieces):
                cols = slice(k * width, (k + 1) * width)
                back = psum.tile([P, width], F32, name="back%d_%d" % (t, k), tag="bank%d" % (7 * (1 - k)))
                for c in range(blocks):
                    nc.tensor.transpose(back[:, c * P:(c + 1) * P], total[:, k * width + c * P:k * width + (c + 1) * P], ident[:])
                nc.scalar.activation(res[t][:, cols], back[:], COPY, scale=-1.0)
                nc.scalar.dma_start(out_rows[t][:, :, cols], res[t][:, cols])

        fetch5(0)
        for t in range(last):
            if t + 1 < last:
                fetch5(t + 1)
            finish_by_transposes(t)

        u = keep.tile([P, N], F32, name="u")
        v = keep.tile([P, N], F32, name="v")
        w = keep.tile([P, N], F32, name="w")
        nc.vector.tensor_tensor(u[:], sw[last][:].indirect(l5[:]), plain[:], ALU.subtract)
        for cols, lcols in halves:
            nc.vector.tensor_tensor(v[:, cols], sw[last][:].indirect(l6[:, lcols]), plain[:, cols], ALU.subtract)
        for cols, lcols in halves:
            nc.vector.tensor_tensor(w[:, cols], u[:, cols], v[:, cols], ALU.max)
        for cols, lcols in halves:
            nc.vector.tensor_tensor(res[last][:, cols], sw[last][:].indirect(l4[:, lcols]), w[:, cols], ALU.subtract)
            nc.sync.dma_start(out_rows[last][:, :, cols], res[last][:, cols])
